import numpy as np
import ml_dtypes


def mxq(x, axis, fmt="e4m3"):
    dtype, down = {"e4m3": (ml_dtypes.float8_e4m3fn, 7), "e5m2": (ml_dtypes.float8_e5m2, 14)}[fmt]
    v = np.moveaxis(np.asarray(x, np.float32).astype(ml_dtypes.bfloat16).astype(np.float64), axis, -1)
    blocks = v.reshape(v.shape[:-1] + (-1, 32))
    amax = np.abs(blocks).max(-1, keepdims=True)
    byte = np.maximum(np.where(amax > 0, np.frexp(amax)[1] - 1 + 127, 0) - down, 1)
    scale = np.exp2(byte - 127.0)
    codes = (blocks / scale).astype(np.float32).astype(dtype).astype(np.float64)
    return np.moveaxis((codes * scale).reshape(v.shape), -1, axis)


WIDE = False


def mx_kscale(k):
    if not WIDE:
        return np.ones(k)
    levels = np.array([18, -18])
    if k % 512:
        return np.exp2(np.random.permutation(np.resize(levels, k // 32))).repeat(32)
    a = np.empty((k // 512, 16))
    for p in range(k // 512):
        a[p, :8] = np.random.permutation(np.resize(levels, 8))
        for g in range(8):
            far = levels[np.abs(levels - a[p, g]) >= 10]
            a[p, g + 8] = far[np.random.randint(len(far))]
    return np.exp2(a.ravel()).repeat(32)


def f64(x):
    return np.asarray(x).astype(np.float64)


def striped(idx):
    return np.tile(np.asarray(idx).reshape(-1, 16).T, (8, 1)).astype(np.uint16)


def unstriped(offs):
    return offs[:16].T.reshape(-1).astype(np.int64)

def planes(y):
    n, m = y.shape
    v = y.astype(np.float32).astype(ml_dtypes.bfloat16).astype(np.float64).reshape(n // 32, 32, m)
    top = np.abs(v).max(1)
    byte = np.clip(np.where(top > 0, np.frexp(top)[1] - 1 + 127 - 7, 1), 1, 254)
    codes = (v * np.exp2(127.0 - byte)[:, None, :]).reshape(n, m).astype(np.float32).astype(ml_dtypes.float8_e4m3fn).view(np.uint8)
    words = codes.reshape(n // 512, 128, 4, m).transpose(0, 1, 3, 2)
    return np.ascontiguousarray(words), np.ascontiguousarray(byte.astype(np.uint8).reshape(n // 512, 16, m))


def setup_inputs():
    n = np.random.standard_normal
    uni = np.random.uniform
    dst = np.random.permutation(np.repeat(np.arange(512), 2))
    inn = np.argsort(dst, kind="stable")
    lea = np.random.permutation(1024)
    f_m = mx_kscale(512)
    return {
        "dyT": (np.round(n((512, 512)) * 8) / 8 * f_m[:, None]).astype(np.float32),
        "hE": (np.round(np.tanh(2.0 * n((512, 1024))) * 256) / 256).astype(np.float32),
        "ws": (n((512, 512)) / np.sqrt(512) / f_m[:, None]).astype(np.float32),
        "wtt": (n((512, 512)) / np.sqrt(512) / f_m[:, None]).astype(np.float32),
        "dstoffs": striped(dst),
        "innoffs": striped(inn),
        "leaoffs": striped(lea),
    }


def reference(dyT, hE, ws, wtt, dstoffs, innoffs, leaoffs):
    dst = unstriped(dstoffs)
    inn = unstriped(innoffs)
    lea = unstriped(leaoffs)
    dyT_c = f64(dyT)[:, dst]
    dz = dyT_c * (1.0 - np.square(f64(hE)))
    q_dz = mxq(dz, 0, "e5m2")
    u = mxq(f64(ws), 0, "e4m3").T @ q_dz
    v = mxq(f64(wtt), 0, "e4m3").T @ q_dz
    u_yo = u[:, lea]
    v_yinn = v[:, inn]
    us_ = u_yo.reshape(512, 512, 2).sum(-1)
    vs_ = v_yinn.reshape(512, 512, 2).sum(-1)
    out_0 = us_ + vs_
    return (out_0,) + planes(out_0)

@@ -1,0 +1,189 @@
+from contextlib import ExitStack
+
+import concourse.mybir as mybir
+
+F32 = mybir.dt.float32
+BF16 = mybir.dt.bfloat16
+I32 = mybir.dt.int32
+U32 = mybir.dt.uint32
+U16 = mybir.dt.uint16
+U8 = mybir.dt.uint8
+E4M3 = mybir.dt.float8_e4m3fn_x4
+E5M2 = mybir.dt.float8_e5m2_x4
+ALU = mybir.AluOpType
+ACT = mybir.ActivationFunctionType
+
+P = 128
+PACK = 4
+M = 512
+DF = 512
+NODES = 512
+EDGES = 1024
+HALF = 512
+QUARTER = 256
+XH = 256
+FLOPS = 2 * 2 * M * DF * EDGES
+
+
+def tile_attend_gedge_tnh_pl_kernel(tc, dyT, hE, ws, wtt, dstoffs, innoffs, leaoffs, out_0, out_1, out_2):
+    nc = tc.nc
+    with ExitStack() as ctx:
+        lists = ctx.enter_context(tc.tile_pool(name="lists", bufs=1))
+        keep = ctx.enter_context(tc.tile_pool(name="keep", bufs=1))
+        psum = ctx.enter_context(tc.psum_pool(name="psum", bufs=8))
+
+        dst = lists.tile([P, EDGES // 16], U16, name="dst")
+        lea = lists.tile([P, EDGES // 16], U16, name="lea")
+        inn = lists.tile([P, EDGES // 16], U16, name="inn")
+
+        dy_rows = dyT.rearrange("(p t) x -> p t x", t=PACK)
+        h_rows = hE.rearrange("(p t) c -> p t c", t=PACK)
+        out_rows = out_0.rearrange("(p j) x -> p j x", j=PACK)
+
+        SPARE = 16
+        dy = [keep.tile([P, NODES + SPARE], F32, name="dy%d" % t) for t in range(PACK)]
+        h_first = [keep.tile([P, HALF], F32, name="h_first%d" % t) for t in range(PACK)]
+        h_second = [keep.tile([P, 2, HALF], F32, name="h_second%d" % u) for u in range(2)]
+        ws_raw = keep.tile([P, PACK, DF], F32, name="ws_raw")
+        wt_raw = keep.tile([P, PACK, DF], F32, name="wt_raw")
+
+        for t in range(PACK):
+            nc.gpsimd.memset(dy[t][:, NODES:], 0.0)
+        warm = keep.tile([P, 8], F32, name="warm")
+        warm2 = keep.tile([P, 8], F32, name="warm2")
+        nc.vector.memset(warm[:], 1.0)
+        nc.scalar.activation(warm2[:], warm[:], ACT.Square)
+
+        nc.sync.dma_start(h_first[0][:], h_rows[:, 0, 0:HALF])
+        nc.sync.dma_start(dst[:], dstoffs)
+        nc.sync.dma_start(dy[0][:, 0:NODES], dy_rows[:, 0, :])
+        for t in range(1, PACK):
+            nc.sync.dma_start(h_first[t][:], h_rows[:, t, 0:HALF])
+            nc.sync.dma_start(dy[t][:, 0:NODES], dy_rows[:, t, :])
+        for u in range(2):
+            nc.sync.dma_start(h_second[u][:], h_rows[:, 2 * u : 2 * u + 2, HALF:EDGES])
+        nc.sync.dma_start(ws_raw[:], ws.rearrange("(p t) d -> p t d", t=PACK))
+        nc.sync.dma_start(wt_raw[:], wtt.rearrange("(p t) d -> p t d", t=PACK))
+        nc.sync.dma_start(lea[:], leaoffs)
+        nc.sync.dma_start(inn[:], innoffs)
+
+        sq = keep.tile([P, PACK, EDGES], F32, name="sq")
+        slope = keep.tile([P, PACK, EDGES], F32, name="slope")
+        dz = keep.tile([P, PACK, EDGES], F32, name="dz")
+        dz_words = [keep.tile([P, HALF * PACK], BF16, name="dz_words%d" % hf, tag="grp%d" % hf, align_bytes=64) for hf in range(2)]
+        dz_codes = [keep.tile([P, HALF], U32, name="dz_codes%d" % hf, align_bytes=64) for hf in range(2)]
+        dz_scales = [keep.tile([P, HALF], U8, name="dz_scales%d" % hf, align_bytes=64) for hf in range(2)]
+
+        def derivative(planes, cols, h_ap):
+            nc.scalar.activation(sq[:, planes, cols], h_ap, ACT.Square)
+            nc.scalar.activation(slope[:, planes, cols], sq[:, planes, cols], ACT.Copy, bias=1.0, scale=-1.0)
+
+        def gather_dz(t, c0, n):
+            nc.vector.tensor_tensor(
+                dz[:, t, c0 : c0 + n], dy[t][:].indirect(dst[:, c0 // 16 : (c0 + n) // 16]), slope[:, t, c0 : c0 + n], ALU.mult
+            )
+
+        def weave(copy, dest, src):
+            copy(dest.rearrange("p (c i t) -> p c t i", i=4, t=PACK), src.rearrange("p t (c i) -> p c t i", i=4))
+
+        def deal(dest, raw):
+            nc.vector.tensor_copy(
+                dest.rearrange("p (j m t) -> p m j t", j=PACK, t=PACK), raw.rearrange("p t (m j) -> p m j t", j=PACK)
+            )
+
+        nc.scalar.activation(sq[:, 0, 0:HALF], h_first[0][:], ACT.Square)
+        nc.vector.tensor_scalar(slope[:, 0, 0:HALF], sq[:, 0, 0:HALF], -1.0, 1.0, ALU.mult, ALU.add)
+        gather_dz(0, 0, HALF)
+        for t in range(1, PACK):
+            derivative(t, slice(0, HALF), h_first[t][:])
+            gather_dz(t, 0, HALF)
+        for q in range(2):
+            for u in range(2):
+                c0 = HALF + q * QUARTER
+                derivative(slice(2 * u, 2 * u + 2), slice(c0, c0 + QUARTER), h_second[u][:, :, q * QUARTER : (q + 1) * QUARTER])
+                gather_dz(2 * u, c0, QUARTER)
+                gather_dz(2 * u + 1, c0, QUARTER)
+
+        ws_words = keep.tile([P, DF * PACK], BF16, name="ws_words", align_bytes=64)
+        ws_codes = keep.tile([P, DF], U32, name="ws_codes", align_bytes=64)
+        ws_scales = keep.tile([P, DF], U8, name="ws_scales", align_bytes=64)
+        wt_codes = keep.tile([P, DF], U32, name="wt_codes", align_bytes=64)
+        wt_scales = keep.tile([P, DF], U8, name="wt_scales", align_bytes=64)
+
+        def quantize_dz(c0, n):
+            hf, a = divmod(c0, HALF)
+            nc.vector.quantize_mx(
+                dz_codes[hf][:, a : a + n].bitcast(E5M2), dz_scales[hf][:, a : a + n], dz_words[hf][:, a * PACK : (a + n) * PACK]
+            )
+
+        weave(nc.scalar.copy, dz_words[0][:], dz[:, :, 0:HALF])
+        weave(nc.scalar.copy, dz_words[1][:, 0 : QUARTER * PACK], dz[:, :, HALF : HALF + QUARTER])
+        deal(ws_words[:], ws_raw[:])
+        quantize_dz(0, HALF)
+        nc.vector.quantize_mx(ws_codes[:].bitcast(E4M3), ws_scales[:], ws_words[:])
+        weave(nc.vector.tensor_copy, dz_words[1][:, QUARTER * PACK :], dz[:, :, HALF + QUARTER :])
+        quantize_dz(HALF, QUARTER)
+        quantize_dz(HALF + QUARTER, QUARTER)
+
+        U_SPARE = 352
+        u_sb = [keep.tile([P, EDGES + U_SPARE], F32, name="u%d" % j) for j in range(PACK)]
+        v_sb = [keep.tile([P, EDGES + SPARE], F32, name="v%d" % j) for j in range(PACK)]
+        for j in range(PACK):
+            nc.gpsimd.memset(u_sb[j][:, EDGES:], 0.0)
+            nc.gpsimd.memset(v_sb[j][:, EDGES:], 0.0)
+
+        def product(codes, scales, j, dest):
+            cols = slice(j * P, (j + 1) * P)
+            for hf in range(2):
+                bank = psum.tile([P, HALF], F32, name="bank")
+                nc.tensor.matmul_mx(
+                    out=bank[:],
+                    lhsT=codes[:, cols].bitcast(E4M3),
+                    lhsT_scale=scales[:, cols],
+                    rhs=dz_codes[hf][:].bitcast(E5M2),
+                    rhs_scale=dz_scales[hf][:],
+                    start=True,
+                    stop=True,
+                )
+                nc.scalar.copy(dest[:, hf * HALF : (hf + 1) * HALF], bank[:])
+
+        product(ws_codes, ws_scales, 0, u_sb[0])
+        wt_words = keep.tile([P, DF * PACK], BF16, name="wt_words", tag="grp1", align_bytes=64)
+        deal(wt_words[:], wt_raw[:])
+        nc.vector.quantize_mx(wt_codes[:].bitcast(E4M3), wt_scales[:], wt_words[:])
+        product(wt_codes, wt_scales, 0, v_sb[0])
+        for j in range(1, PACK):
+            product(ws_codes, ws_scales, j, u_sb[j])
+            product(wt_codes, wt_scales, j, v_sb[j])
+
+        result = keep.tile([P, PACK, NODES], F32, name="result")
+        out_words = [keep.tile([P, XH * PACK], BF16, name="out_words%d" % xh, align_bytes=64) for xh in range(2)]
+        out_codes = [keep.tile([P, XH], U32, name="out_codes%d" % xh, align_bytes=64) for xh in range(2)]
+        out_scales = keep.tile([P, NODES], U8, name="out_scales", align_bytes=64)
+        words_hbm = out_1.rearrange("a p c l -> p (a c l)").bitcast(I32)
+        scales_hbm = out_2.rearrange("a b c -> (a b) c").bitcast(I32)
+
+        def node_sums(engine, j, x0, n):
+            entries = slice(2 * x0 // 16, 2 * (x0 + n) // 16)
+            picked = keep.tile([P, 2 * n], F32, name="picked", tag="picked%d" % j)
+            both = keep.tile([P, n, 2], F32, name="both", tag="both%d_%d" % (j, x0))
+            nc.vector.tensor_copy(picked[:], u_sb[j][:].indirect(lea[:, entries]))
+            nc.vector.tensor_tensor(both[:].rearrange("p x e -> p (x e)"), v_sb[j][:].indirect(inn[:, entries]), picked[:], ALU.add)
+            engine.tensor_tensor(result[:, j, x0 : x0 + n], both[:, :, 0], both[:, :, 1], ALU.add)
+            nc.sync.dma_start(out_rows[:, j, x0 : x0 + n], result[:, j, x0 : x0 + n])
+
+        def planes(xh):
+            nc.vector.quantize_mx(out_codes[xh][:].bitcast(E4M3), out_scales[:, xh * XH : (xh + 1) * XH], out_words[xh][:])
+            nc.sync.dma_start(words_hbm[:, xh * XH : (xh + 1) * XH], out_codes[xh][:].bitcast(I32))
+
+        for j in range(PACK - 1):
+            node_sums(nc.gpsimd, j, 0, NODES)
+        node_sums(nc.gpsimd, PACK - 1, 0, XH)
+        weave(nc.scalar.copy, out_words[0][:], result[:, :, 0:XH])
+        node_sums(nc.vector, PACK - 1, XH, XH)
+        planes(0)
+        weave(nc.vector.tensor_copy, out_words[1][:], result[:, :, XH:])
+        planes(1)
+        for quad in range(4):
+            queue = nc.sync if quad % 2 == 0 else nc.scalar
+            queue.dma_start(scales_hbm[4 * quad : 4 * quad + 4, :], out_scales[32 * quad : 32 * quad + 4, :].bitcast(I32))

@@ -30,7 +30,7 @@ def tile_attend_gedge_tnh_pl_kernel(tc, dyT, hE, ws, wtt, dstoffs, innoffs, leao
     with ExitStack() as ctx:
         lists = ctx.enter_context(tc.tile_pool(name="lists", bufs=1))
         keep = ctx.enter_context(tc.tile_pool(name="keep", bufs=1))
-        psum = ctx.enter_context(tc.psum_pool(name="psum", bufs=8))
+        psum = ctx.enter_context(tc.psum_pool(name="psum", bufs=1))
 
         dst = lists.tile([P, EDGES // 16], U16, name="dst")
         lea = lists.tile([P, EDGES // 16], U16, name="lea")
@@ -59,71 +59,95 @@ def tile_attend_gedge_tnh_pl_kernel(tc, dyT, hE, ws, wtt, dstoffs, innoffs, leao
         nc.sync.dma_start(dy[0][:, 0:NODES], dy_rows[:, 0, :])
         for t in range(1, PACK):
             nc.sync.dma_start(h_first[t][:], h_rows[:, t, 0:HALF])
+            if t == PACK - 1:
+                nc.sync.dma_start(h_second[0][:], h_rows[:, 0:2, HALF:EDGES])
             nc.sync.dma_start(dy[t][:, 0:NODES], dy_rows[:, t, :])
-        for u in range(2):
-            nc.sync.dma_start(h_second[u][:], h_rows[:, 2 * u : 2 * u + 2, HALF:EDGES])
+        nc.sync.dma_start(h_second[1][:], h_rows[:, 2:4, HALF:EDGES])
         nc.sync.dma_start(ws_raw[:], ws.rearrange("(p t) d -> p t d", t=PACK))
         nc.sync.dma_start(wt_raw[:], wtt.rearrange("(p t) d -> p t d", t=PACK))
         nc.sync.dma_start(lea[:], leaoffs)
         nc.sync.dma_start(inn[:], innoffs)
 
-        sq = keep.tile([P, PACK, EDGES], F32, name="sq")
-        slope = keep.tile([P, PACK, EDGES], F32, name="slope")
-        dz = keep.tile([P, PACK, EDGES], F32, name="dz")
-        dz_words = [keep.tile([P, HALF * PACK], BF16, name="dz_words%d" % hf, tag="grp%d" % hf, align_bytes=64) for hf in range(2)]
+        dz = [keep.tile([P, PACK * HALF], F32, name="dz%d" % hf, align_bytes=64) for hf in range(2)]
+        words_area = keep.tile([P, EDGES * PACK // 2], F32, name="words_area", align_bytes=64)
+        dz_words = words_area[:].bitcast(BF16)
+        ws_area = keep.tile([P, DF * PACK // 2], F32, name="ws_area", align_bytes=64)
+        ws_words = [ws_area[:, 0:HALF].bitcast(BF16), words_area[:, 1280:1792].bitcast(BF16)]
+        wt_words = dz[0][:, 0 : DF * PACK // 2].bitcast(BF16)
         dz_codes = [keep.tile([P, HALF], U32, name="dz_codes%d" % hf, align_bytes=64) for hf in range(2)]
         dz_scales = [keep.tile([P, HALF], U8, name="dz_scales%d" % hf, align_bytes=64) for hf in range(2)]
-
-        def derivative(planes, cols, h_ap):
-            nc.scalar.activation(sq[:, planes, cols], h_ap, ACT.Square)
-            nc.scalar.activation(slope[:, planes, cols], sq[:, planes, cols], ACT.Copy, bias=1.0, scale=-1.0)
-
-        def gather_dz(t, c0, n):
-            nc.vector.tensor_tensor(
-                dz[:, t, c0 : c0 + n], dy[t][:].indirect(dst[:, c0 // 16 : (c0 + n) // 16]), slope[:, t, c0 : c0 + n], ALU.mult
-            )
-
-        def weave(copy, dest, src):
-            copy(dest.rearrange("p (c i t) -> p c t i", i=4, t=PACK), src.rearrange("p t (c i) -> p c t i", i=4))
-
-        def deal(dest, raw):
-            nc.vector.tensor_copy(
-                dest.rearrange("p (j m t) -> p m j t", j=PACK, t=PACK), raw.rearrange("p t (m j) -> p m j t", j=PACK)
-            )
-
-        nc.scalar.activation(sq[:, 0, 0:HALF], h_first[0][:], ACT.Square)
-        nc.vector.tensor_scalar(slope[:, 0, 0:HALF], sq[:, 0, 0:HALF], -1.0, 1.0, ALU.mult, ALU.add)
-        gather_dz(0, 0, HALF)
-        for t in range(1, PACK):
-            derivative(t, slice(0, HALF), h_first[t][:])
-            gather_dz(t, 0, HALF)
-        for q in range(2):
-            for u in range(2):
-                c0 = HALF + q * QUARTER
-                derivative(slice(2 * u, 2 * u + 2), slice(c0, c0 + QUARTER), h_second[u][:, :, q * QUARTER : (q + 1) * QUARTER])
-                gather_dz(2 * u, c0, QUARTER)
-                gather_dz(2 * u + 1, c0, QUARTER)
-
-        ws_words = keep.tile([P, DF * PACK], BF16, name="ws_words", align_bytes=64)
         ws_codes = keep.tile([P, DF], U32, name="ws_codes", align_bytes=64)
         ws_scales = keep.tile([P, DF], U8, name="ws_scales", align_bytes=64)
         wt_codes = keep.tile([P, DF], U32, name="wt_codes", align_bytes=64)
         wt_scales = keep.tile([P, DF], U8, name="wt_scales", align_bytes=64)
 
+        def square(dest, h_ap):
+            nc.scalar.activation(dest, h_ap, ACT.Square)
+
+        def one_minus(dest, src):
+            nc.scalar.activation(dest, src, ACT.Copy, bias=1.0, scale=-1.0)
+
+        def gather_dz(t, c0, n, slope):
+            hf, a = divmod(c0, HALF)
+            nc.vector.tensor_tensor(
+                dz[hf][:, t * HALF + a : t * HALF + a + n], dy[t][:].indirect(dst[:, c0 // 16 : (c0 + n) // 16]), slope, ALU.mult
+            )
+
+        def weave_dz(copy, c0, n):
+            hf, a = divmod(c0, HALF)
+            weave(copy, dz_words[:, c0 * PACK : (c0 + n) * PACK], dz[hf][:].rearrange("p (t c) -> p t c", t=PACK)[:, :, a : a + n])
+
+        def weave(copy, dest, src):
+            copy(dest.rearrange("p (c i t) -> p c t i", i=4, t=PACK), src.rearrange("p t (c i) -> p c t i", i=4))
+
+        def deal(copy, dest, raw, j0, nj):
+            copy(dest.rearrange("p (j m t) -> p m j t", j=nj, t=PACK), raw.rearrange("p t (m j) -> p m j t", j=PACK)[:, :, j0 : j0 + nj, :])
+
+        def quantize_ws(u):
+            cols = slice(2 * u * P, 2 * (u + 1) * P)
+            nc.vector.quantize_mx(ws_codes[:, cols].bitcast(E4M3), ws_scales[:, cols], ws_words[u])
+
         def quantize_dz(c0, n):
             hf, a = divmod(c0, HALF)
             nc.vector.quantize_mx(
-                dz_codes[hf][:, a : a + n].bitcast(E5M2), dz_scales[hf][:, a : a + n], dz_words[hf][:, a * PACK : (a + n) * PACK]
+                dz_codes[hf][:, a : a + n].bitcast(E5M2), dz_scales[hf][:, a : a + n], dz_words[:, c0 * PACK : (c0 + n) * PACK]
             )
 
-        weave(nc.scalar.copy, dz_words[0][:], dz[:, :, 0:HALF])
-        weave(nc.scalar.copy, dz_words[1][:, 0 : QUARTER * PACK], dz[:, :, HALF : HALF + QUARTER])
-        deal(ws_words[:], ws_raw[:])
+        for t in range(PACK):
+            sq = keep.tile([P, HALF], F32, name="sq_first%d" % t)
+            slope = keep.tile([P, HALF], F32, name="slope_first%d" % t)
+            square(sq[:], h_first[t][:])
+            if t < 2:
+                nc.vector.tensor_scalar(slope[:], sq[:], -1.0, 1.0, ALU.mult, ALU.add)
+            else:
+                one_minus(slope[:], sq[:])
+            gather_dz(t, 0, HALF, slope[:])
+
+        sq_second = keep.tile([P, 3 * HALF], F32, name="sq_second")
+        slope_second = keep.tile([P, 2 * HALF], F32, name="slope_second")
+        slope_q = [ws_area[:, 0:HALF], ws_area[:, HALF:]]
+        for t in range(2):
+            square(sq_second[:, t * HALF : (t + 1) * HALF], h_second[0][:, t, :])
+        for t in range(2):
+            one_minus(slope_second[:, t * HALF : (t + 1) * HALF], sq_second[:, t * HALF : (t + 1) * HALF])
+            gather_dz(t, HALF, HALF, slope_second[:, t * HALF : (t + 1) * HALF])
+        sq_q = [sq_second[:, 2 * HALF :], words_area[:, 768:1280]]
+        for q in range(2):
+            square(sq_q[q].rearrange("p (t c) -> p t c", t=2), h_second[1][:, :, q * QUARTER : (q + 1) * QUARTER])
+        for q in range(2):
+            one_minus(slope_q[q], sq_q[q])
+            for t in range(2):
+                gather_dz(2 + t, HALF + q * QUARTER, QUARTER, slope_q[q][:, t * QUARTER : (t + 1) * QUARTER])
+
+        weave_dz(nc.scalar.copy, 0, HALF)
+        weave_dz(nc.scalar.copy, HALF, QUARTER)
+        deal(nc.scalar.copy, wt_words, wt_raw[:], 0, PACK)
+        deal(nc.vector.tensor_copy, ws_words[0], ws_raw[:], 0, 2)
+        weave_dz(nc.vector.tensor_copy, HALF + QUARTER, QUARTER)
+        quantize_ws(0)
         quantize_dz(0, HALF)
-        nc.vector.quantize_mx(ws_codes[:].bitcast(E4M3), ws_scales[:], ws_words[:])
-        weave(nc.vector.tensor_copy, dz_words[1][:, QUARTER * PACK :], dz[:, :, HALF + QUARTER :])
-        quantize_dz(HALF, QUARTER)
         quantize_dz(HALF + QUARTER, QUARTER)
+        quantize_dz(HALF, QUARTER)
 
         U_SPARE = 352
         u_sb = [keep.tile([P, EDGES + U_SPARE], F32, name="u%d" % j) for j in range(PACK)]
@@ -132,29 +156,35 @@ def tile_attend_gedge_tnh_pl_kernel(tc, dyT, hE, ws, wtt, dstoffs, innoffs, leao
             nc.gpsimd.memset(u_sb[j][:, EDGES:], 0.0)
             nc.gpsimd.memset(v_sb[j][:, EDGES:], 0.0)
 
-        def product(codes, scales, j, dest):
-            cols = slice(j * P, (j + 1) * P)
-            for hf in range(2):
-                bank = psum.tile([P, HALF], F32, name="bank")
-                nc.tensor.matmul_mx(
-                    out=bank[:],
-                    lhsT=codes[:, cols].bitcast(E4M3),
-                    lhsT_scale=scales[:, cols],
-                    rhs=dz_codes[hf][:].bitcast(E5M2),
-                    rhs_scale=dz_scales[hf][:],
-                    start=True,
-                    stop=True,
-                )
-                nc.scalar.copy(dest[:, hf * HALF : (hf + 1) * HALF], bank[:])
+        banks = [psum.tile([P, HALF], F32, name="bank%d" % b) for b in range(3)]
 
-        product(ws_codes, ws_scales, 0, u_sb[0])
-        wt_words = keep.tile([P, DF * PACK], BF16, name="wt_words", tag="grp1", align_bytes=64)
-        deal(wt_words[:], wt_raw[:])
-        nc.vector.quantize_mx(wt_codes[:].bitcast(E4M3), wt_scales[:], wt_words[:])
-        product(wt_codes, wt_scales, 0, v_sb[0])
-        for j in range(1, PACK):
-            product(ws_codes, ws_scales, j, u_sb[j])
-            product(wt_codes, wt_scales, j, v_sb[j])
+        def product(codes, scales, j, dest, hf, bank):
+            cols = slice(j * P, (j + 1) * P)
+            nc.tensor.matmul_mx(
+                out=bank[:],
+                lhsT=codes[:, cols].bitcast(E4M3),
+                lhsT_scale=scales[:, cols],
+                rhs=dz_codes[hf][:].bitcast(E5M2),
+                rhs_scale=dz_scales[hf][:],
+                start=True,
+                stop=True,
+            )
+            nc.scalar.copy(dest[:, hf * HALF : (hf + 1) * HALF], bank[:])
+
+        product(ws_codes, ws_scales, 0, u_sb[0], 0, banks[0])
+        product(ws_codes, ws_scales, 0, u_sb[0], 1, banks[1])
+        product(ws_codes, ws_scales, 1, u_sb[1], 1, banks[2])
+        product(ws_codes, ws_scales, 1, u_sb[1], 0, banks[1])
+        deal(nc.vector.tensor_copy, ws_words[1], ws_raw[:], 2, 2)
+        nc.vector.quantize_mx(wt_codes[:].bitcast(E4M3), wt_scales[:], wt_words)
+        quantize_ws(1)
+        rest = []
+        for j in range(PACK):
+            rest.append((wt_codes, wt_scales, j, v_sb[j]))
+            if j + 2 < PACK:
+                rest.append((ws_codes, ws_scales, j + 2, u_sb[j + 2]))
+        for k in range(2 * len(rest)):
+            product(*rest[k // 2], k % 2, banks[(-k) % 3])
 
         result = keep.tile([P, PACK, NODES], F32, name="result")
         out_words = [keep.tile([P, XH * PACK], BF16, name="out_words%d" % xh, align_bytes=64) for xh in range(2)]
@@ -162,27 +192,42 @@ def tile_attend_gedge_tnh_pl_kernel(tc, dyT, hE, ws, wtt, dstoffs, innoffs, leao
         out_scales = keep.tile([P, NODES], U8, name="out_scales", align_bytes=64)
         words_hbm = out_1.rearrange("a p c l -> p (a c l)").bitcast(I32)
         scales_hbm = out_2.rearrange("a b c -> (a b) c").bitcast(I32)
+        picked = [keep.tile([P, EDGES], F32, name="picked%d" % j) for j in range(PACK)]
+        both = [keep.tile([P, EDGES], F32, name="both%d" % j) for j in range(PACK)]
 
-        def node_sums(engine, j, x0, n):
-            entries = slice(2 * x0 // 16, 2 * (x0 + n) // 16)
-            picked = keep.tile([P, 2 * n], F32, name="picked", tag="picked%d" % j)
-            both = keep.tile([P, n, 2], F32, name="both", tag="both%d_%d" % (j, x0))
-            nc.vector.tensor_copy(picked[:], u_sb[j][:].indirect(lea[:, entries]))
-            nc.vector.tensor_tensor(both[:].rearrange("p x e -> p (x e)"), v_sb[j][:].indirect(inn[:, entries]), picked[:], ALU.add)
-            engine.tensor_tensor(result[:, j, x0 : x0 + n], both[:, :, 0], both[:, :, 1], ALU.add)
+        def gather_u(j, e0, n, dest):
+            nc.vector.tensor_copy(dest, u_sb[j][:].indirect(lea[:, e0 // 16 : (e0 + n) // 16]))
+
+        def gather_v(j, e0, n, src):
+            nc.vector.tensor_tensor(both[j][:, e0 : e0 + n], v_sb[j][:].indirect(inn[:, e0 // 16 : (e0 + n) // 16]), src, ALU.add)
+
+        def pair_sums(engine, j, x0, n):
+            pairs = both[j][:, 2 * x0 : 2 * (x0 + n)].rearrange("p (x e) -> p x e", e=2)
+            engine.tensor_tensor(result[:, j, x0 : x0 + n], pairs[:, :, 0], pairs[:, :, 1], ALU.add)
             nc.sync.dma_start(out_rows[:, j, x0 : x0 + n], result[:, j, x0 : x0 + n])
 
         def planes(xh):
             nc.vector.quantize_mx(out_codes[xh][:].bitcast(E4M3), out_scales[:, xh * XH : (xh + 1) * XH], out_words[xh][:])
             nc.sync.dma_start(words_hbm[:, xh * XH : (xh + 1) * XH], out_codes[xh][:].bitcast(I32))
 
-        for j in range(PACK - 1):
-            node_sums(nc.gpsimd, j, 0, NODES)
-        node_sums(nc.gpsimd, PACK - 1, 0, XH)
+        gather_u(0, 0, EDGES, picked[0][:])
+        gather_u(1, 0, EDGES, picked[1][:])
+        gather_v(0, 0, EDGES, picked[0][:])
+        pair_sums(nc.gpsimd, 0, 0, NODES)
+        gather_u(2, 0, EDGES, picked[2][:])
+        gather_v(1, 0, EDGES, picked[1][:])
+        pair_sums(nc.gpsimd, 1, 0, NODES)
+        gather_u(3, 0, HALF, picked[3][:, 0:HALF])
+        gather_v(2, 0, EDGES, picked[2][:])
+        pair_sums(nc.gpsimd, 2, 0, NODES)
+        gather_u(3, HALF, HALF, picked[2][:, 0:HALF])
+        gather_v(3, 0, HALF, picked[3][:, 0:HALF])
+        gather_v(3, HALF, HALF, picked[2][:, 0:HALF])
+        pair_sums(nc.vector, 3, 0, XH)
         weave(nc.scalar.copy, out_words[0][:], result[:, :, 0:XH])
-        node_sums(nc.vector, PACK - 1, XH, XH)
-        planes(0)
+        pair_sums(nc.vector, 3, XH, XH)
         weave(nc.vector.tensor_copy, out_words[1][:], result[:, :, XH:])
+        planes(0)
         planes(1)
         for quad in range(4):
             queue = nc.sync if quad % 2 == 0 else nc.scalar

@@ -1,6 +1,7 @@
 from contextlib import ExitStack
 
 import concourse.mybir as mybir
+from concourse.masks import make_identity
 
 F32 = mybir.dt.float32
 BF16 = mybir.dt.bfloat16
@@ -43,7 +44,8 @@ def tile_attend_gedge_tnh_pl_kernel(tc, dyT, hE, ws, wtt, dstoffs, innoffs, leao
         SPARE = 16
         dy = [keep.tile([P, NODES + SPARE], F32, name="dy%d" % t) for t in range(PACK)]
         h_first = [keep.tile([P, HALF], F32, name="h_first%d" % t) for t in range(PACK)]
-        h_second = [keep.tile([P, 2, HALF], F32, name="h_second%d" % u) for u in range(2)]
+        h_second = [keep.tile([P, HALF], F32, name="h_second%d" % t) for t in range(2)]
+        h_last = keep.tile([P, 2, HALF], F32, name="h_last")
         ws_raw = keep.tile([P, PACK, DF], F32, name="ws_raw")
         wt_raw = keep.tile([P, PACK, DF], F32, name="wt_raw")
 
@@ -54,15 +56,15 @@ def tile_attend_gedge_tnh_pl_kernel(tc, dyT, hE, ws, wtt, dstoffs, innoffs, leao
         nc.vector.memset(warm[:], 1.0)
         nc.scalar.activation(warm2[:], warm[:], ACT.Square)
 
-        nc.sync.dma_start(h_first[0][:], h_rows[:, 0, 0:HALF])
+        h_pieces = [(h_first[t][:], h_rows[:, t, 0:HALF]) for t in range(PACK)]
+        h_pieces = h_pieces + [(h_second[t][:], h_rows[:, t, HALF:EDGES]) for t in range(2)]
+        nc.sync.dma_start(*h_pieces[0])
+        nc.sync.dma_start(*h_pieces[1])
         nc.sync.dma_start(dst[:], dstoffs)
-        nc.sync.dma_start(dy[0][:, 0:NODES], dy_rows[:, 0, :])
-        for t in range(1, PACK):
-            nc.sync.dma_start(h_first[t][:], h_rows[:, t, 0:HALF])
-            if t == PACK - 1:
-                nc.sync.dma_start(h_second[0][:], h_rows[:, 0:2, HALF:EDGES])
+        for t in range(PACK):
             nc.sync.dma_start(dy[t][:, 0:NODES], dy_rows[:, t, :])
-        nc.sync.dma_start(h_second[1][:], h_rows[:, 2:4, HALF:EDGES])
+            nc.sync.dma_start(*h_pieces[t + 2])
+        nc.sync.dma_start(h_last[:], h_rows[:, 2:4, HALF:EDGES])
         nc.sync.dma_start(ws_raw[:], ws.rearrange("(p t) d -> p t d", t=PACK))
         nc.sync.dma_start(wt_raw[:], wtt.rearrange("(p t) d -> p t d", t=PACK))
         nc.sync.dma_start(lea[:], leaoffs)
@@ -73,7 +75,7 @@ def tile_attend_gedge_tnh_pl_kernel(tc, dyT, hE, ws, wtt, dstoffs, innoffs, leao
         dz_words = words_area[:].bitcast(BF16)
         ws_area = keep.tile([P, DF * PACK // 2], F32, name="ws_area", align_bytes=64)
         ws_words = [ws_area[:, 0:HALF].bitcast(BF16), words_area[:, 1280:1792].bitcast(BF16)]
-        wt_words = dz[0][:, 0 : DF * PACK // 2].bitcast(BF16)
+        wt_words = dz[0][:, 0:HALF].bitcast(BF16)
         dz_codes = [keep.tile([P, HALF], U32, name="dz_codes%d" % hf, align_bytes=64) for hf in range(2)]
         dz_scales = [keep.tile([P, HALF], U8, name="dz_scales%d" % hf, align_bytes=64) for hf in range(2)]
         ws_codes = keep.tile([P, DF], U32, name="ws_codes", align_bytes=64)
@@ -113,11 +115,18 @@ def tile_attend_gedge_tnh_pl_kernel(tc, dyT, hE, ws, wtt, dstoffs, innoffs, leao
                 dz_codes[hf][:, a : a + n].bitcast(E5M2), dz_scales[hf][:, a : a + n], dz_words[:, c0 * PACK : (c0 + n) * PACK]
             )
 
+        def quantize_wt(u):
+            cols = slice(2 * u * P, 2 * (u + 1) * P)
+            nc.vector.quantize_mx(wt_codes[:, cols].bitcast(E4M3), wt_scales[:, cols], wt_words)
+
+        ident = keep.tile([P, P], F32, name="ident")
+        make_identity(nc, ident[:])
+
         for t in range(PACK):
             sq = keep.tile([P, HALF], F32, name="sq_first%d" % t)
             slope = keep.tile([P, HALF], F32, name="slope_first%d" % t)
             square(sq[:], h_first[t][:])
-            if t < 2:
+            if t == 0:
                 nc.vector.tensor_scalar(slope[:], sq[:], -1.0, 1.0, ALU.mult, ALU.add)
             else:
                 one_minus(slope[:], sq[:])
@@ -127,13 +136,13 @@ def tile_attend_gedge_tnh_pl_kernel(tc, dyT, hE, ws, wtt, dstoffs, innoffs, leao
         slope_second = keep.tile([P, 2 * HALF], F32, name="slope_second")
         slope_q = [ws_area[:, 0:HALF], ws_area[:, HALF:]]
         for t in range(2):
-            square(sq_second[:, t * HALF : (t + 1) * HALF], h_second[0][:, t, :])
+            square(sq_second[:, t * HALF : (t + 1) * HALF], h_second[t][:])
         for t in range(2):
             one_minus(slope_second[:, t * HALF : (t + 1) * HALF], sq_second[:, t * HALF : (t + 1) * HALF])
             gather_dz(t, HALF, HALF, slope_second[:, t * HALF : (t + 1) * HALF])
         sq_q = [sq_second[:, 2 * HALF :], words_area[:, 768:1280]]
         for q in range(2):
-            square(sq_q[q].rearrange("p (t c) -> p t c", t=2), h_second[1][:, :, q * QUARTER : (q + 1) * QUARTER])
+            square(sq_q[q].rearrange("p (t c) -> p t c", t=2), h_last[:, :, q * QUARTER : (q + 1) * QUARTER])
         for q in range(2):
             one_minus(slope_q[q], sq_q[q])
             for t in range(2):
@@ -141,7 +150,7 @@ def tile_attend_gedge_tnh_pl_kernel(tc, dyT, hE, ws, wtt, dstoffs, innoffs, leao
 
         weave_dz(nc.scalar.copy, 0, HALF)
         weave_dz(nc.scalar.copy, HALF, QUARTER)
-        deal(nc.scalar.copy, wt_words, wt_raw[:], 0, PACK)
+        deal(nc.scalar.copy, wt_words, wt_raw[:], 0, 2)
         deal(nc.vector.tensor_copy, ws_words[0], ws_raw[:], 0, 2)
         weave_dz(nc.vector.tensor_copy, HALF + QUARTER, QUARTER)
         quantize_ws(0)
@@ -174,17 +183,18 @@ def tile_attend_gedge_tnh_pl_kernel(tc, dyT, hE, ws, wtt, dstoffs, innoffs, leao
         product(ws_codes, ws_scales, 0, u_sb[0], 0, banks[0])
         product(ws_codes, ws_scales, 0, u_sb[0], 1, banks[1])
         product(ws_codes, ws_scales, 1, u_sb[1], 1, banks[2])
-        product(ws_codes, ws_scales, 1, u_sb[1], 0, banks[1])
+        product(ws_codes, ws_scales, 1, u_sb[1], 0, banks[0])
         deal(nc.vector.tensor_copy, ws_words[1], ws_raw[:], 2, 2)
-        nc.vector.quantize_mx(wt_codes[:].bitcast(E4M3), wt_scales[:], wt_words)
+        quantize_wt(0)
         quantize_ws(1)
-        rest = []
-        for j in range(PACK):
-            rest.append((wt_codes, wt_scales, j, v_sb[j]))
-            if j + 2 < PACK:
-                rest.append((ws_codes, ws_scales, j + 2, u_sb[j + 2]))
+        deal(nc.scalar.copy, wt_words, wt_raw[:], 2, 2)
+        quantize_wt(1)
+        product(wt_codes, wt_scales, 0, v_sb[0], 0, banks[1])
+        product(wt_codes, wt_scales, 0, v_sb[0], 1, banks[2])
+        rest = [(ws_codes, ws_scales, 2, u_sb[2]), (wt_codes, wt_scales, 1, v_sb[1]), (wt_codes, wt_scales, 2, v_sb[2])]
+        rest = rest + [(ws_codes, ws_scales, 3, u_sb[3]), (wt_codes, wt_scales, 3, v_sb[3])]
         for k in range(2 * len(rest)):
-            product(*rest[k // 2], k % 2, banks[(-k) % 3])
+            product(*rest[k // 2], k % 2, banks[k % 3])
 
         result = keep.tile([P, PACK, NODES], F32, name="result")
         out_words = [keep.tile([P, XH * PACK], BF16, name="out_words%d" % xh, align_bytes=64) for xh in range(2)]
@@ -210,19 +220,38 @@ def tile_attend_gedge_tnh_pl_kernel(tc, dyT, hE, ws, wtt, dstoffs, innoffs, leao
             nc.vector.quantize_mx(out_codes[xh][:].bitcast(E4M3), out_scales[:, xh * XH : (xh + 1) * XH], out_words[xh][:])
             nc.sync.dma_start(words_hbm[:, xh * XH : (xh + 1) * XH], out_codes[xh][:].bitcast(I32))
 
+        summed = banks[0]
+        back = psum.tile([P, NODES], F32, name="back")
+
+        def pair_sums_tensor(j):
+            turned = keep.tile([P, NODES], F32, name="turned%d" % j)
+            for b in range(NODES // P):
+                for e in range(2):
+                    nc.tensor.matmul(
+                        summed[:, b * P : (b + 1) * P],
+                        lhsT=both[j][:, 2 * b * P + e : 2 * (b + 1) * P : 2],
+                        rhs=ident[:],
+                        start=(e == 0),
+                        stop=(e == 1),
+                        is_transpose=True,
+                    )
+            nc.scalar.copy(turned[:], summed[:])
+            for b in range(NODES // P):
+                nc.tensor.transpose(back[:, b * P : (b + 1) * P], turned[:, b * P : (b + 1) * P], ident[:])
+            nc.scalar.copy(result[:, j, :], back[:])
+            nc.scalar.dma_start(out_rows[:, j, :], result[:, j, :])
+
         gather_u(0, 0, EDGES, picked[0][:])
         gather_u(1, 0, EDGES, picked[1][:])
-        gather_v(0, 0, EDGES, picked[0][:])
-        pair_sums(nc.gpsimd, 0, 0, NODES)
-        gather_u(2, 0, EDGES, picked[2][:])
-        gather_v(1, 0, EDGES, picked[1][:])
-        pair_sums(nc.gpsimd, 1, 0, NODES)
+        for j in range(PACK - 1):
+            gather_v(j, 0, EDGES, picked[j][:])
+            pair_sums_tensor(j)
+            if j == 0:
+                gather_u(2, 0, EDGES, picked[2][:])
         gather_u(3, 0, HALF, picked[3][:, 0:HALF])
-        gather_v(2, 0, EDGES, picked[2][:])
-        pair_sums(nc.gpsimd, 2, 0, NODES)
-        gather_u(3, HALF, HALF, picked[2][:, 0:HALF])
+        gather_u(3, HALF, HALF, picked[3][:, HALF:])
         gather_v(3, 0, HALF, picked[3][:, 0:HALF])
-        gather_v(3, HALF, HALF, picked[2][:, 0:HALF])
+        gather_v(3, HALF, HALF, picked[3][:, HALF:])
         pair_sums(nc.vector, 3, 0, XH)
         weave(nc.scalar.copy, out_words[0][:], result[:, :, 0:XH])
         pair_sums(nc.vector, 3, XH, XH)

@@ -15,15 +15,20 @@ ALU = mybir.AluOpType
 ACT = mybir.ActivationFunctionType
 
 P = 128
-PACK = 4
-M = 512
-DF = 512
+PLANES = 4
+LAST = PLANES - 1
+MESSAGE_FEATURES = 512
+NODE_FEATURES = 512
 NODES = 512
 EDGES = 1024
-HALF = 512
-QUARTER = 256
-XH = 256
-FLOPS = 2 * 2 * M * DF * EDGES
+HALF = EDGES // 2
+QUARTER = EDGES // 4
+NODE_HALF = NODES // 2
+ENTRIES_PER_COLUMN = 16
+LINE = 4
+SPARE = 16
+U_SPARE = 352
+FLOPS = 2 * 2 * MESSAGE_FEATURES * NODE_FEATURES * EDGES
 
 
 def tile_attend_gedge_tnh_pl_kernel(tc, dyT, hE, ws, wtt, dstoffs, innoffs, leaoffs, out_0, out_1, out_2):
@@ -33,231 +38,260 @@ def tile_attend_gedge_tnh_pl_kernel(tc, dyT, hE, ws, wtt, dstoffs, innoffs, leao
         keep = ctx.enter_context(tc.tile_pool(name="keep", bufs=1))
         psum = ctx.enter_context(tc.psum_pool(name="psum", bufs=1))
 
-        dst = lists.tile([P, EDGES // 16], U16, name="dst")
-        lea = lists.tile([P, EDGES // 16], U16, name="lea")
-        inn = lists.tile([P, EDGES // 16], U16, name="inn")
+        def entries(list_tile, first, count):
+            return list_tile[:, first // ENTRIES_PER_COLUMN : (first + count) // ENTRIES_PER_COLUMN]
 
-        dy_rows = dyT.rearrange("(p t) x -> p t x", t=PACK)
-        h_rows = hE.rearrange("(p t) c -> p t c", t=PACK)
-        out_rows = out_0.rearrange("(p j) x -> p j x", j=PACK)
-
-        SPARE = 16
-        dy = [keep.tile([P, NODES + SPARE], F32, name="dy%d" % t) for t in range(PACK)]
-        h_first = [keep.tile([P, HALF], F32, name="h_first%d" % t) for t in range(PACK)]
-        h_second = [keep.tile([P, HALF], F32, name="h_second%d" % t) for t in range(2)]
-        h_last = keep.tile([P, 2, HALF], F32, name="h_last")
-        ws_raw = keep.tile([P, PACK, DF], F32, name="ws_raw")
-        wt_raw = keep.tile([P, PACK, DF], F32, name="wt_raw")
-
-        for t in range(PACK):
-            nc.gpsimd.memset(dy[t][:, NODES:], 0.0)
-        warm = keep.tile([P, 8], F32, name="warm")
-        warm2 = keep.tile([P, 8], F32, name="warm2")
-        nc.vector.memset(warm[:], 1.0)
-        nc.scalar.activation(warm2[:], warm[:], ACT.Square)
-
-        h_pieces = [(h_first[t][:], h_rows[:, t, 0:HALF]) for t in range(PACK)]
-        h_pieces = h_pieces + [(h_second[t][:], h_rows[:, t, HALF:EDGES]) for t in range(2)]
-        nc.sync.dma_start(*h_pieces[0])
-        nc.sync.dma_start(*h_pieces[1])
-        nc.sync.dma_start(dst[:], dstoffs)
-        for t in range(PACK):
-            nc.sync.dma_start(dy[t][:, 0:NODES], dy_rows[:, t, :])
-            nc.sync.dma_start(*h_pieces[t + 2])
-        nc.sync.dma_start(h_last[:], h_rows[:, 2:4, HALF:EDGES])
-        nc.sync.dma_start(ws_raw[:], ws.rearrange("(p t) d -> p t d", t=PACK))
-        nc.sync.dma_start(wt_raw[:], wtt.rearrange("(p t) d -> p t d", t=PACK))
-        nc.sync.dma_start(lea[:], leaoffs)
-        nc.sync.dma_start(inn[:], innoffs)
-
-        dz = [keep.tile([P, PACK * HALF], F32, name="dz%d" % hf, align_bytes=64) for hf in range(2)]
-        words_area = keep.tile([P, EDGES * PACK // 2], F32, name="words_area", align_bytes=64)
-        dz_words = words_area[:].bitcast(BF16)
-        ws_area = keep.tile([P, DF * PACK // 2], F32, name="ws_area", align_bytes=64)
-        ws_words = [ws_area[:, 0:HALF].bitcast(BF16), words_area[:, 1280:1792].bitcast(BF16)]
-        wt_words = dz[0][:, 0:HALF].bitcast(BF16)
-        dz_codes = [keep.tile([P, HALF], U32, name="dz_codes%d" % hf, align_bytes=64) for hf in range(2)]
-        dz_scales = [keep.tile([P, HALF], U8, name="dz_scales%d" % hf, align_bytes=64) for hf in range(2)]
-        ws_codes = keep.tile([P, DF], U32, name="ws_codes", align_bytes=64)
-        ws_scales = keep.tile([P, DF], U8, name="ws_scales", align_bytes=64)
-        wt_codes = keep.tile([P, DF], U32, name="wt_codes", align_bytes=64)
-        wt_scales = keep.tile([P, DF], U8, name="wt_scales", align_bytes=64)
-
-        def square(dest, h_ap):
-            nc.scalar.activation(dest, h_ap, ACT.Square)
-
-        def one_minus(dest, src):
-            nc.scalar.activation(dest, src, ACT.Copy, bias=1.0, scale=-1.0)
-
-        def gather_dz(t, c0, n, slope):
-            hf, a = divmod(c0, HALF)
-            nc.vector.tensor_tensor(
-                dz[hf][:, t * HALF + a : t * HALF + a + n], dy[t][:].indirect(dst[:, c0 // 16 : (c0 + n) // 16]), slope, ALU.mult
+        def weave(copy, words, planes):
+            copy(
+                words.rearrange("p (c i t) -> p c t i", i=LINE, t=PLANES),
+                planes.rearrange("p t (c i) -> p c t i", i=LINE),
             )
 
-        def weave_dz(copy, c0, n):
-            hf, a = divmod(c0, HALF)
-            weave(copy, dz_words[:, c0 * PACK : (c0 + n) * PACK], dz[hf][:].rearrange("p (t c) -> p t c", t=PACK)[:, :, a : a + n])
+        def deal(copy, words, weights, pair):
+            dealt = weights.rearrange("p t (r j) -> p r j t", j=PLANES)[:, :, 2 * pair : 2 * pair + 2, :]
+            copy(words.rearrange("p (j r t) -> p r j t", j=2, t=PLANES), dealt)
 
-        def weave(copy, dest, src):
-            copy(dest.rearrange("p (c i t) -> p c t i", i=4, t=PACK), src.rearrange("p t (c i) -> p c t i", i=4))
+        dst = lists.tile([P, EDGES // ENTRIES_PER_COLUMN], U16, name="dst")
+        lea = lists.tile([P, EDGES // ENTRIES_PER_COLUMN], U16, name="lea")
+        inn = lists.tile([P, EDGES // ENTRIES_PER_COLUMN], U16, name="inn")
+        dy_rows = dyT.rearrange("(p t) x -> p t x", t=PLANES)
+        h_rows = hE.rearrange("(p t) c -> p t c", t=PLANES)
+        dy = [keep.tile([P, NODES + SPARE], F32, name="dy%d" % t) for t in range(PLANES)]
+        h_low = [[keep.tile([P, HALF], F32, name="h%d_%d" % (t, hf)) for hf in range(2)] for t in range(2)]
+        h_high = keep.tile([P, 2, EDGES], F32, name="h_high")
+        ws_raw = keep.tile([P, PLANES, NODE_FEATURES], F32, name="ws_raw")
+        wt_raw = keep.tile([P, PLANES, NODE_FEATURES], F32, name="wt_raw")
+        u_planes = [keep.tile([P, EDGES + U_SPARE * (j < LAST)], F32, name="u%d" % j) for j in range(PLANES)]
+        v_planes = [keep.tile([P, EDGES + SPARE * (j < LAST)], F32, name="v%d" % j) for j in range(PLANES)]
 
-        def deal(copy, dest, raw, j0, nj):
-            copy(dest.rearrange("p (j m t) -> p m j t", j=nj, t=PACK), raw.rearrange("p t (m j) -> p m j t", j=PACK)[:, :, j0 : j0 + nj, :])
-
-        def quantize_ws(u):
-            cols = slice(2 * u * P, 2 * (u + 1) * P)
-            nc.vector.quantize_mx(ws_codes[:, cols].bitcast(E4M3), ws_scales[:, cols], ws_words[u])
-
-        def quantize_dz(c0, n):
-            hf, a = divmod(c0, HALF)
-            nc.vector.quantize_mx(
-                dz_codes[hf][:, a : a + n].bitcast(E5M2), dz_scales[hf][:, a : a + n], dz_words[:, c0 * PACK : (c0 + n) * PACK]
-            )
-
-        def quantize_wt(u):
-            cols = slice(2 * u * P, 2 * (u + 1) * P)
-            nc.vector.quantize_mx(wt_codes[:, cols].bitcast(E4M3), wt_scales[:, cols], wt_words)
-
+        one_set = keep.tile([P, 1], F32, name="one_set")
+        one = keep.tile([P, 1], F32, name="one")
+        nc.vector.memset(one_set[:], 1.0)
+        nc.scalar.activation(one[:], one_set[:], ACT.Square)
+        for t in range(PLANES):
+            nc.vector.memset(dy[t][:, NODES:], 0.0)
+        for j in range(LAST):
+            nc.vector.memset(u_planes[j][:, EDGES:], 0.0)
+            nc.vector.memset(v_planes[j][:, EDGES:], 0.0)
         ident = keep.tile([P, P], F32, name="ident")
         make_identity(nc, ident[:])
 
-        for t in range(PACK):
-            sq = keep.tile([P, HALF], F32, name="sq_first%d" % t)
-            slope = keep.tile([P, HALF], F32, name="slope_first%d" % t)
-            square(sq[:], h_first[t][:])
-            if t == 0:
-                nc.vector.tensor_scalar(slope[:], sq[:], -1.0, 1.0, ALU.mult, ALU.add)
-            else:
-                one_minus(slope[:], sq[:])
-            gather_dz(t, 0, HALF, slope[:])
+        def load_dy(t):
+            nc.sync.dma_start(dy[t][:, 0:NODES], dy_rows[:, t, :])
 
-        sq_second = keep.tile([P, 3 * HALF], F32, name="sq_second")
-        slope_second = keep.tile([P, 2 * HALF], F32, name="slope_second")
-        slope_q = [ws_area[:, 0:HALF], ws_area[:, HALF:]]
         for t in range(2):
-            square(sq_second[:, t * HALF : (t + 1) * HALF], h_second[t][:])
+            for hf in range(2):
+                nc.sync.dma_start(h_low[t][hf][:], h_rows[:, t, hf * HALF : (hf + 1) * HALF])
+            if t == 0:
+                nc.sync.dma_start(dst[:], dstoffs)
+            load_dy(t)
         for t in range(2):
-            one_minus(slope_second[:, t * HALF : (t + 1) * HALF], sq_second[:, t * HALF : (t + 1) * HALF])
-            gather_dz(t, HALF, HALF, slope_second[:, t * HALF : (t + 1) * HALF])
-        sq_q = [sq_second[:, 2 * HALF :], words_area[:, 768:1280]]
+            nc.sync.dma_start(h_high[:, t, 0:HALF], h_rows[:, 2 + t, 0:HALF])
+        load_dy(2)
+        nc.sync.dma_start(h_high[:, :, HALF:], h_rows[:, 2:4, HALF:])
+        load_dy(3)
+        nc.sync.dma_start(ws_raw[:], ws.rearrange("(p t) d -> p t d", t=PLANES))
+        nc.sync.dma_start(wt_raw[:], wtt.rearrange("(p t) d -> p t d", t=PLANES))
+        nc.sync.dma_start(lea[:], leaoffs)
+        nc.sync.dma_start(inn[:], innoffs)
+
+        dz = [keep.tile([P, PLANES * HALF], F32, name="dz%d" % hf) for hf in range(2)]
+        dz_codes = [keep.tile([P, HALF], U32, name="dz_codes%d" % hf, align_bytes=64) for hf in range(2)]
+        dz_scales = [keep.tile([P, HALF], U8, name="dz_scales%d" % hf, align_bytes=64) for hf in range(2)]
+        ws_codes = keep.tile([P, NODE_FEATURES], U32, name="ws_codes", align_bytes=64)
+        ws_scales = keep.tile([P, NODE_FEATURES], U8, name="ws_scales", align_bytes=64)
+        wt_codes = keep.tile([P, NODE_FEATURES], U32, name="wt_codes", align_bytes=64)
+        wt_scales = keep.tile([P, NODE_FEATURES], U8, name="wt_scales", align_bytes=64)
+
+        room = QUARTER * PLANES // 2
+        stage = keep.tile([P, 3 * room], F32, name="stage", align_bytes=64)
+        stage_words = stage[:].bitcast(BF16)
+        wt_words = stage[:, 0:room].bitcast(BF16)
+        ws_stage = keep.tile([P, room + QUARTER], F32, name="ws_stage", align_bytes=64)
+        ws_words = [ws_stage[:, 0:room].bitcast(BF16), stage[:, 2 * room :].bitcast(BF16)]
+
+        squares_tile = keep.tile([P, 7, HALF], F32, name="squares_tile")
+        slopes_tile = keep.tile([P, 7, HALF], F32, name="slopes_tile")
+        across = 2 * room - HALF // 2
+        squares = [squares_tile[:, k, :] for k in range(6)] + [stage[:, across : across + HALF], squares_tile[:, 6, :]]
+        slopes = [slopes_tile[:, k, :] for k in range(6)] + [ws_stage[:, room - QUARTER :], slopes_tile[:, 6, :]]
+
+        def make_square(piece, h_values):
+            nc.scalar.activation(piece, h_values, ACT.Square)
+
+        def make_slope(k):
+            nc.scalar.activation(slopes[k], squares[k], ACT.Identity, bias=one[:], scale=-1.0)
+
+        def gather_dz(t, first, count, slope):
+            hf, at = divmod(first, HALF)
+            window = dy[t][:].indirect(entries(dst, first, count))
+            nc.vector.tensor_tensor(dz[hf][:, t * HALF + at : t * HALF + at + count], window, slope, ALU.mult)
+
+        def dz_words(first, count):
+            at = first % (3 * QUARTER)
+            return stage_words[:, at * PLANES : (at + count) * PLANES]
+
+        def weave_dz(copy, first, count):
+            hf, at = divmod(first, HALF)
+            weave(copy, dz_words(first, count), dz[hf][:].rearrange("p (t c) -> p t c", t=PLANES)[:, :, at : at + count])
+
+        def quantize_dz(quarter):
+            hf, at = divmod(quarter * QUARTER, HALF)
+            cols = slice(at, at + QUARTER)
+            nc.vector.quantize_mx(dz_codes[hf][:, cols].bitcast(E5M2), dz_scales[hf][:, cols], dz_words(quarter * QUARTER, QUARTER))
+
+        def quantize_pair(codes, scales, pair, words):
+            cols = slice(2 * pair * P, 2 * (pair + 1) * P)
+            nc.vector.quantize_mx(codes[:, cols].bitcast(E4M3), scales[:, cols], words)
+
+        make_square(squares[0], h_low[0][0][:])
+        nc.vector.tensor_scalar(slopes[0], squares[0], -1.0, 1.0, ALU.mult, ALU.add)
+        make_square(squares[1], h_low[0][1][:])
+        make_slope(1)
+        for hf in range(2):
+            gather_dz(0, hf * HALF, HALF, slopes[hf])
+        for hf in range(2):
+            make_square(squares[2 + hf], h_low[1][hf][:])
+        for hf in range(2):
+            make_slope(2 + hf)
+            gather_dz(1, hf * HALF, HALF, slopes[2 + hf])
+        for t in range(2):
+            make_square(squares[4 + t], h_high[:, t, 0:HALF])
+            make_slope(4 + t)
+            gather_dz(2 + t, 0, HALF, slopes[4 + t])
         for q in range(2):
-            square(sq_q[q].rearrange("p (t c) -> p t c", t=2), h_last[:, :, q * QUARTER : (q + 1) * QUARTER])
-        for q in range(2):
-            one_minus(slope_q[q], sq_q[q])
+            first = HALF + q * QUARTER
+            make_square(squares[6 + q].rearrange("p (t c) -> p t c", t=2), h_high[:, :, first : first + QUARTER])
+
+        def gather_quarter(q):
             for t in range(2):
-                gather_dz(2 + t, HALF + q * QUARTER, QUARTER, slope_q[q][:, t * QUARTER : (t + 1) * QUARTER])
+                gather_dz(2 + t, HALF + q * QUARTER, QUARTER, slopes[6 + q][:, t * QUARTER : (t + 1) * QUARTER])
+
+        make_slope(6)
+        gather_quarter(0)
+        make_slope(7)
+        deal(nc.vector.tensor_copy, ws_words[0], ws_raw[:], 0)
+        gather_quarter(1)
 
         weave_dz(nc.scalar.copy, 0, HALF)
         weave_dz(nc.scalar.copy, HALF, QUARTER)
-        deal(nc.scalar.copy, wt_words, wt_raw[:], 0, 2)
-        deal(nc.vector.tensor_copy, ws_words[0], ws_raw[:], 0, 2)
+        quantize_pair(ws_codes, ws_scales, 0, ws_words[0])
+        quantize_dz(0)
+        quantize_dz(1)
         weave_dz(nc.vector.tensor_copy, HALF + QUARTER, QUARTER)
-        quantize_ws(0)
-        quantize_dz(0, HALF)
-        quantize_dz(HALF + QUARTER, QUARTER)
-        quantize_dz(HALF, QUARTER)
+        quantize_dz(2)
+        quantize_dz(3)
 
-        U_SPARE = 352
-        u_sb = [keep.tile([P, EDGES + U_SPARE], F32, name="u%d" % j) for j in range(PACK)]
-        v_sb = [keep.tile([P, EDGES + SPARE], F32, name="v%d" % j) for j in range(PACK)]
-        for j in range(PACK):
-            nc.gpsimd.memset(u_sb[j][:, EDGES:], 0.0)
-            nc.gpsimd.memset(v_sb[j][:, EDGES:], 0.0)
+        banks = [psum.tile([P, HALF], F32, name="bank%d" % b) for b in range(4)]
 
-        banks = [psum.tile([P, HALF], F32, name="bank%d" % b) for b in range(3)]
-
-        def product(codes, scales, j, dest, hf, bank):
+        def product(codes, scales, j, plane, first_bank):
             cols = slice(j * P, (j + 1) * P)
-            nc.tensor.matmul_mx(
-                out=bank[:],
-                lhsT=codes[:, cols].bitcast(E4M3),
-                lhsT_scale=scales[:, cols],
-                rhs=dz_codes[hf][:].bitcast(E5M2),
-                rhs_scale=dz_scales[hf][:],
-                start=True,
-                stop=True,
-            )
-            nc.scalar.copy(dest[:, hf * HALF : (hf + 1) * HALF], bank[:])
+            for hf in range(2):
+                bank = banks[first_bank + hf]
+                nc.tensor.matmul_mx(
+                    out=bank[:],
+                    lhsT=codes[:, cols].bitcast(E4M3),
+                    lhsT_scale=scales[:, cols],
+                    rhs=dz_codes[hf][:].bitcast(E5M2),
+                    rhs_scale=dz_scales[hf][:],
+                    start=True,
+                    stop=True,
+                )
+                nc.scalar.copy(plane[:, hf * HALF : (hf + 1) * HALF], bank[:])
 
-        product(ws_codes, ws_scales, 0, u_sb[0], 0, banks[0])
-        product(ws_codes, ws_scales, 0, u_sb[0], 1, banks[1])
-        product(ws_codes, ws_scales, 1, u_sb[1], 1, banks[2])
-        product(ws_codes, ws_scales, 1, u_sb[1], 0, banks[0])
-        deal(nc.vector.tensor_copy, ws_words[1], ws_raw[:], 2, 2)
-        quantize_wt(0)
-        quantize_ws(1)
-        deal(nc.scalar.copy, wt_words, wt_raw[:], 2, 2)
-        quantize_wt(1)
-        product(wt_codes, wt_scales, 0, v_sb[0], 0, banks[1])
-        product(wt_codes, wt_scales, 0, v_sb[0], 1, banks[2])
-        rest = [(ws_codes, ws_scales, 2, u_sb[2]), (wt_codes, wt_scales, 1, v_sb[1]), (wt_codes, wt_scales, 2, v_sb[2])]
-        rest = rest + [(ws_codes, ws_scales, 3, u_sb[3]), (wt_codes, wt_scales, 3, v_sb[3])]
-        for k in range(2 * len(rest)):
-            product(*rest[k // 2], k % 2, banks[k % 3])
+        def product_u(j, first_bank):
+            product(ws_codes, ws_scales, j, u_planes[j], first_bank)
 
-        result = keep.tile([P, PACK, NODES], F32, name="result")
-        out_words = [keep.tile([P, XH * PACK], BF16, name="out_words%d" % xh, align_bytes=64) for xh in range(2)]
-        out_codes = [keep.tile([P, XH], U32, name="out_codes%d" % xh, align_bytes=64) for xh in range(2)]
-        out_scales = keep.tile([P, NODES], U8, name="out_scales", align_bytes=64)
+        def product_v(j, first_bank):
+            product(wt_codes, wt_scales, j, v_planes[j], first_bank)
+
+        product_u(0, 0)
+        product_u(1, 2)
+        deal(nc.vector.tensor_copy, ws_words[1], ws_raw[:], 1)
+        deal(nc.vector.tensor_copy, wt_words, wt_raw[:], 0)
+        quantize_pair(ws_codes, ws_scales, 1, ws_words[1])
+        quantize_pair(wt_codes, wt_scales, 0, wt_words)
+        deal(nc.scalar.copy, wt_words, wt_raw[:], 1)
+        quantize_pair(wt_codes, wt_scales, 1, wt_words)
+        product_v(0, 0)
+        product_u(2, 2)
+        product_v(1, 0)
+        product_v(2, 2)
+        product_u(3, 0)
+        product_v(3, 2)
+
+        out_rows = out_0.rearrange("(p j) x -> p j x", j=PLANES)
         words_hbm = out_1.rearrange("a p c l -> p (a c l)").bitcast(I32)
         scales_hbm = out_2.rearrange("a b c -> (a b) c").bitcast(I32)
-        picked = [keep.tile([P, EDGES], F32, name="picked%d" % j) for j in range(PACK)]
-        both = [keep.tile([P, EDGES], F32, name="both%d" % j) for j in range(PACK)]
-
-        def gather_u(j, e0, n, dest):
-            nc.vector.tensor_copy(dest, u_sb[j][:].indirect(lea[:, e0 // 16 : (e0 + n) // 16]))
-
-        def gather_v(j, e0, n, src):
-            nc.vector.tensor_tensor(both[j][:, e0 : e0 + n], v_sb[j][:].indirect(inn[:, e0 // 16 : (e0 + n) // 16]), src, ALU.add)
-
-        def pair_sums(engine, j, x0, n):
-            pairs = both[j][:, 2 * x0 : 2 * (x0 + n)].rearrange("p (x e) -> p x e", e=2)
-            engine.tensor_tensor(result[:, j, x0 : x0 + n], pairs[:, :, 0], pairs[:, :, 1], ALU.add)
-            nc.sync.dma_start(out_rows[:, j, x0 : x0 + n], result[:, j, x0 : x0 + n])
-
-        def planes(xh):
-            nc.vector.quantize_mx(out_codes[xh][:].bitcast(E4M3), out_scales[:, xh * XH : (xh + 1) * XH], out_words[xh][:])
-            nc.sync.dma_start(words_hbm[:, xh * XH : (xh + 1) * XH], out_codes[xh][:].bitcast(I32))
-
-        summed = banks[0]
+        result = keep.tile([P, PLANES, NODES], F32, name="result")
+        out_words = [keep.tile([P, NODE_HALF * PLANES], BF16, name="out_words%d" % xh, align_bytes=64) for xh in range(2)]
+        out_codes = [keep.tile([P, NODE_HALF], U32, name="out_codes%d" % xh, align_bytes=64) for xh in range(2)]
+        out_scales = keep.tile([P, NODES], U8, name="out_scales", align_bytes=64)
+        picked = [keep.tile([P, EDGES], F32, name="picked%d" % j) for j in range(PLANES)]
+        both = [keep.tile([P, EDGES], F32, name="both%d" % j) for j in range(PLANES)]
         back = psum.tile([P, NODES], F32, name="back")
 
-        def pair_sums_tensor(j):
+        def gather_u(j, first, count):
+            window = u_planes[j][:].indirect(entries(lea, first, count))
+            nc.vector.tensor_copy(picked[j][:, first : first + count], window)
+
+        def gather_v(j, first, count):
+            window = v_planes[j][:].indirect(entries(inn, first, count))
+            nc.vector.tensor_tensor(both[j][:, first : first + count], window, picked[j][:, first : first + count], ALU.add)
+
+        def add_pairs_on_tensor(j):
             turned = keep.tile([P, NODES], F32, name="turned%d" % j)
-            for b in range(NODES // P):
+            summed = banks[2 + j % 2]
+            for block in range(NODES // P):
                 for e in range(2):
                     nc.tensor.matmul(
-                        summed[:, b * P : (b + 1) * P],
-                        lhsT=both[j][:, 2 * b * P + e : 2 * (b + 1) * P : 2],
+                        summed[:, block * P : (block + 1) * P],
+                        lhsT=both[j][:, 2 * block * P + e : 2 * (block + 1) * P : 2],
                         rhs=ident[:],
                         start=(e == 0),
                         stop=(e == 1),
                         is_transpose=True,
                     )
             nc.scalar.copy(turned[:], summed[:])
-            for b in range(NODES // P):
-                nc.tensor.transpose(back[:, b * P : (b + 1) * P], turned[:, b * P : (b + 1) * P], ident[:])
+            for block in range(NODES // P):
+                cols = slice(block * P, (block + 1) * P)
+                nc.tensor.transpose(back[:, cols], turned[:, cols], ident[:])
             nc.scalar.copy(result[:, j, :], back[:])
-            nc.scalar.dma_start(out_rows[:, j, :], result[:, j, :])
 
-        gather_u(0, 0, EDGES, picked[0][:])
-        gather_u(1, 0, EDGES, picked[1][:])
-        for j in range(PACK - 1):
-            gather_v(j, 0, EDGES, picked[j][:])
-            pair_sums_tensor(j)
-            if j == 0:
-                gather_u(2, 0, EDGES, picked[2][:])
-        gather_u(3, 0, HALF, picked[3][:, 0:HALF])
-        gather_u(3, HALF, HALF, picked[3][:, HALF:])
-        gather_v(3, 0, HALF, picked[3][:, 0:HALF])
-        gather_v(3, HALF, HALF, picked[3][:, HALF:])
-        pair_sums(nc.vector, 3, 0, XH)
-        weave(nc.scalar.copy, out_words[0][:], result[:, :, 0:XH])
-        pair_sums(nc.vector, 3, XH, XH)
-        weave(nc.vector.tensor_copy, out_words[1][:], result[:, :, XH:])
-        planes(0)
-        planes(1)
-        for quad in range(4):
-            queue = nc.sync if quad % 2 == 0 else nc.scalar
-            queue.dma_start(scales_hbm[4 * quad : 4 * quad + 4, :], out_scales[32 * quad : 32 * quad + 4, :].bitcast(I32))
+        def finish_nodes(xh):
+            nodes = slice(xh * NODE_HALF, (xh + 1) * NODE_HALF)
+            pairs = both[LAST][:].rearrange("p (x e) -> p x e", e=2)[:, nodes, :]
+            nc.vector.tensor_tensor(result[:, LAST, nodes], pairs[:, :, 0], pairs[:, :, 1], ALU.add)
+            nc.sync.dma_start(out_rows[:, 2:4, nodes], result[:, 2:4, nodes])
+
+        def store_planes(xh):
+            nodes = slice(xh * NODE_HALF, (xh + 1) * NODE_HALF)
+            nc.vector.quantize_mx(out_codes[xh][:].bitcast(E4M3), out_scales[:, nodes], out_words[xh][:])
+            nc.sync.dma_start(words_hbm[:, nodes], out_codes[xh][:].bitcast(I32))
+
+        gather_u(0, 0, EDGES)
+        gather_u(1, 0, EDGES)
+        gather_v(0, 0, EDGES)
+        add_pairs_on_tensor(0)
+        nc.sync.dma_start(out_rows[:, 0, :], result[:, 0, :])
+        gather_u(2, 0, EDGES)
+        gather_v(1, 0, EDGES)
+        add_pairs_on_tensor(1)
+        nc.sync.dma_start(out_rows[:, 1, :], result[:, 1, :])
+        gather_v(2, 0, EDGES)
+        add_pairs_on_tensor(2)
+        for gather in (gather_u, gather_v):
+            for xh in range(2):
+                gather(LAST, xh * HALF, HALF)
+
+        for xh, copy in enumerate((nc.scalar.copy, nc.vector.tensor_copy)):
+            finish_nodes(xh)
+            weave(copy, out_words[xh][:], result[:, :, xh * NODE_HALF : (xh + 1) * NODE_HALF])
+        for xh in range(2):
+            store_planes(xh)
+        for quadrant in range(4):
+            queue = nc.sync if quadrant % 2 == 0 else nc.scalar
+            queue.dma_start(
+                scales_hbm[4 * quadrant : 4 * quadrant + 4, :],
+                out_scales[32 * quadrant : 32 * quadrant + 4, :].bitcast(I32),
+            )

from contextlib import ExitStack

import concourse.mybir as mybir
from concourse.masks import make_identity

F32 = mybir.dt.float32
BF16 = mybir.dt.bfloat16
I32 = mybir.dt.int32
U32 = mybir.dt.uint32
U16 = mybir.dt.uint16
U8 = mybir.dt.uint8
E4M3 = mybir.dt.float8_e4m3fn_x4
E5M2 = mybir.dt.float8_e5m2_x4
ALU = mybir.AluOpType
ACT = mybir.ActivationFunctionType

P = 128
PLANES = 4
LAST = PLANES - 1
MESSAGE_FEATURES = 512
NODE_FEATURES = 512
NODES = 512
EDGES = 1024
HALF = EDGES // 2
QUARTER = EDGES // 4
NODE_HALF = NODES // 2
ENTRIES_PER_COLUMN = 16
LINE = 4
SPARE = 16
U_SPARE = 352
FLOPS = 2 * 2 * MESSAGE_FEATURES * NODE_FEATURES * EDGES


def tile_attend_gedge_tnh_pl_kernel(tc, dyT, hE, ws, wtt, dstoffs, innoffs, leaoffs, out_0, out_1, out_2):
    nc = tc.nc
    with ExitStack() as ctx:
        lists = ctx.enter_context(tc.tile_pool(name="lists", bufs=1))
        keep = ctx.enter_context(tc.tile_pool(name="keep", bufs=1))
        psum = ctx.enter_context(tc.psum_pool(name="psum", bufs=1))

        def entries(list_tile, first, count):
            return list_tile[:, first // ENTRIES_PER_COLUMN : (first + count) // ENTRIES_PER_COLUMN]

        def weave(copy, words, planes):
            copy(
                words.rearrange("p (c i t) -> p c t i", i=LINE, t=PLANES),
                planes.rearrange("p t (c i) -> p c t i", i=LINE),
            )

        def deal(copy, words, weights, pair):
            dealt = weights.rearrange("p t (r j) -> p r j t", j=PLANES)[:, :, 2 * pair : 2 * pair + 2, :]
            copy(words.rearrange("p (j r t) -> p r j t", j=2, t=PLANES), dealt)

        dst = lists.tile([P, EDGES // ENTRIES_PER_COLUMN], U16, name="dst")
        lea = lists.tile([P, EDGES // ENTRIES_PER_COLUMN], U16, name="lea")
        inn = lists.tile([P, EDGES // ENTRIES_PER_COLUMN], U16, name="inn")
        dy_rows = dyT.rearrange("(p t) x -> p t x", t=PLANES)
        h_rows = hE.rearrange("(p t) c -> p t c", t=PLANES)
        dy = [keep.tile([P, NODES + SPARE], F32, name="dy%d" % t) for t in range(PLANES)]
        h_low = [[keep.tile([P, HALF], F32, name="h%d_%d" % (t, hf)) for hf in range(2)] for t in range(2)]
        h_high = keep.tile([P, 2, EDGES], F32, name="h_high")
        ws_raw = keep.tile([P, PLANES, NODE_FEATURES], F32, name="ws_raw")
        wt_raw = keep.tile([P, PLANES, NODE_FEATURES], F32, name="wt_raw")
        u_planes = [keep.tile([P, EDGES + U_SPARE * (j < LAST)], F32, name="u%d" % j) for j in range(PLANES)]
        v_planes = [keep.tile([P, EDGES + SPARE * (j < LAST)], F32, name="v%d" % j) for j in range(PLANES)]

        one_set = keep.tile([P, 1], F32, name="one_set")
        one = keep.tile([P, 1], F32, name="one")
        nc.vector.memset(one_set[:], 1.0)
        nc.scalar.activation(one[:], one_set[:], ACT.Square)
        for t in range(PLANES):
            nc.vector.memset(dy[t][:, NODES:], 0.0)
        for j in range(LAST):
            nc.vector.memset(u_planes[j][:, EDGES:], 0.0)
            nc.vector.memset(v_planes[j][:, EDGES:], 0.0)
        ident = keep.tile([P, P], F32, name="ident")
        make_identity(nc, ident[:])

        def load_dy(t):
            nc.sync.dma_start(dy[t][:, 0:NODES], dy_rows[:, t, :])

        for t in range(2):
            for hf in range(2):
                nc.sync.dma_start(h_low[t][hf][:], h_rows[:, t, hf * HALF : (hf + 1) * HALF])
            if t == 0:
                nc.sync.dma_start(dst[:], dstoffs)
            load_dy(t)
        for t in range(2):
            nc.sync.dma_start(h_high[:, t, 0:HALF], h_rows[:, 2 + t, 0:HALF])
        load_dy(2)
        nc.sync.dma_start(h_high[:, :, HALF:], h_rows[:, 2:4, HALF:])
        load_dy(3)
        nc.sync.dma_start(ws_raw[:], ws.rearrange("(p t) d -> p t d", t=PLANES))
        nc.sync.dma_start(wt_raw[:], wtt.rearrange("(p t) d -> p t d", t=PLANES))
        nc.sync.dma_start(lea[:], leaoffs)
        nc.sync.dma_start(inn[:], innoffs)

        dz = [keep.tile([P, PLANES * HALF], F32, name="dz%d" % hf) for hf in range(2)]
        dz_codes = [keep.tile([P, HALF], U32, name="dz_codes%d" % hf, align_bytes=64) for hf in range(2)]
        dz_scales = [keep.tile([P, HALF], U8, name="dz_scales%d" % hf, align_bytes=64) for hf in range(2)]
        ws_codes = keep.tile([P, NODE_FEATURES], U32, name="ws_codes", align_bytes=64)
        ws_scales = keep.tile([P, NODE_FEATURES], U8, name="ws_scales", align_bytes=64)
        wt_codes = keep.tile([P, NODE_FEATURES], U32, name="wt_codes", align_bytes=64)
        wt_scales = keep.tile([P, NODE_FEATURES], U8, name="wt_scales", align_bytes=64)

        room = QUARTER * PLANES // 2
        stage = keep.tile([P, 3 * room], F32, name="stage", align_bytes=64)
        stage_words = stage[:].bitcast(BF16)
        wt_words = stage[:, 0:room].bitcast(BF16)
        ws_stage = keep.tile([P, room + QUARTER], F32, name="ws_stage", align_bytes=64)
        ws_words = [ws_stage[:, 0:room].bitcast(BF16), stage[:, 2 * room :].bitcast(BF16)]

        squares_tile = keep.tile([P, 7, HALF], F32, name="squares_tile")
        slopes_tile = keep.tile([P, 7, HALF], F32, name="slopes_tile")
        across = 2 * room - HALF // 2
        squares = [squares_tile[:, k, :] for k in range(6)] + [stage[:, across : across + HALF], squares_tile[:, 6, :]]
        slopes = [slopes_tile[:, k, :] for k in range(6)] + [ws_stage[:, room - QUARTER :], slopes_tile[:, 6, :]]

        def make_square(piece, h_values):
            nc.scalar.activation(piece, h_values, ACT.Square)

        def make_slope(k):
            nc.scalar.activation(slopes[k], squares[k], ACT.Identity, bias=one[:], scale=-1.0)

        def gather_dz(t, first, count, slope):
            hf, at = divmod(first, HALF)
            window = dy[t][:].indirect(entries(dst, first, count))
            nc.vector.tensor_tensor(dz[hf][:, t * HALF + at : t * HALF + at + count], window, slope, ALU.mult)

        def dz_words(first, count):
            at = first % (3 * QUARTER)
            return stage_words[:, at * PLANES : (at + count) * PLANES]

        def weave_dz(copy, first, count):
            hf, at = divmod(first, HALF)
            weave(copy, dz_words(first, count), dz[hf][:].rearrange("p (t c) -> p t c", t=PLANES)[:, :, at : at + count])

        def quantize_dz(quarter):
            hf, at = divmod(quarter * QUARTER, HALF)
            cols = slice(at, at + QUARTER)
            nc.vector.quantize_mx(dz_codes[hf][:, cols].bitcast(E5M2), dz_scales[hf][:, cols], dz_words(quarter * QUARTER, QUARTER))

        def quantize_pair(codes, scales, pair, words):
            cols = slice(2 * pair * P, 2 * (pair + 1) * P)
            nc.vector.quantize_mx(codes[:, cols].bitcast(E4M3), scales[:, cols], words)

        make_square(squares[0], h_low[0][0][:])
        nc.vector.tensor_scalar(slopes[0], squares[0], -1.0, 1.0, ALU.mult, ALU.add)
        make_square(squares[1], h_low[0][1][:])
        make_slope(1)
        for hf in range(2):
            gather_dz(0, hf * HALF, HALF, slopes[hf])
        for hf in range(2):
            make_square(squares[2 + hf], h_low[1][hf][:])
        for hf in range(2):
            make_slope(2 + hf)
            gather_dz(1, hf * HALF, HALF, slopes[2 + hf])
        for t in range(2):
            make_square(squares[4 + t], h_high[:, t, 0:HALF])
            make_slope(4 + t)
            gather_dz(2 + t, 0, HALF, slopes[4 + t])
        for q in range(2):
            first = HALF + q * QUARTER
            make_square(squares[6 + q].rearrange("p (t c) -> p t c", t=2), h_high[:, :, first : first + QUARTER])

        def gather_quarter(q):
            for t in range(2):
                gather_dz(2 + t, HALF + q * QUARTER, QUARTER, slopes[6 + q][:, t * QUARTER : (t + 1) * QUARTER])

        make_slope(6)
        gather_quarter(0)
        make_slope(7)
        deal(nc.vector.tensor_copy, ws_words[0], ws_raw[:], 0)
        gather_quarter(1)

        weave_dz(nc.scalar.copy, 0, HALF)
        weave_dz(nc.scalar.copy, HALF, QUARTER)
        quantize_pair(ws_codes, ws_scales, 0, ws_words[0])
        quantize_dz(0)
        quantize_dz(1)
        weave_dz(nc.vector.tensor_copy, HALF + QUARTER, QUARTER)
        quantize_dz(2)
        quantize_dz(3)

        banks = [psum.tile([P, HALF], F32, name="bank%d" % b) for b in range(4)]

        def product(codes, scales, j, plane, first_bank):
            cols = slice(j * P, (j + 1) * P)
            for hf in range(2):
                bank = banks[first_bank + hf]
                nc.tensor.matmul_mx(
                    out=bank[:],
                    lhsT=codes[:, cols].bitcast(E4M3),
                    lhsT_scale=scales[:, cols],
                    rhs=dz_codes[hf][:].bitcast(E5M2),
                    rhs_scale=dz_scales[hf][:],
                    start=True,
                    stop=True,
                )
                nc.scalar.copy(plane[:, hf * HALF : (hf + 1) * HALF], bank[:])

        def product_u(j, first_bank):
            product(ws_codes, ws_scales, j, u_planes[j], first_bank)

        def product_v(j, first_bank):
            product(wt_codes, wt_scales, j, v_planes[j], first_bank)

        product_u(0, 0)
        product_u(1, 2)
        deal(nc.vector.tensor_copy, ws_words[1], ws_raw[:], 1)
        deal(nc.vector.tensor_copy, wt_words, wt_raw[:], 0)
        quantize_pair(ws_codes, ws_scales, 1, ws_words[1])
        quantize_pair(wt_codes, wt_scales, 0, wt_words)
        deal(nc.scalar.copy, wt_words, wt_raw[:], 1)
        quantize_pair(wt_codes, wt_scales, 1, wt_words)
        product_v(0, 0)
        product_u(2, 2)
        product_v(1, 0)
        product_v(2, 2)
        product_u(3, 0)
        product_v(3, 2)

        out_rows = out_0.rearrange("(p j) x -> p j x", j=PLANES)
        words_hbm = out_1.rearrange("a p c l -> p (a c l)").bitcast(I32)
        scales_hbm = out_2.rearrange("a b c -> (a b) c").bitcast(I32)
        result = keep.tile([P, PLANES, NODES], F32, name="result")
        out_words = [keep.tile([P, NODE_HALF * PLANES], BF16, name="out_words%d" % xh, align_bytes=64) for xh in range(2)]
        out_codes = [keep.tile([P, NODE_HALF], U32, name="out_codes%d" % xh, align_bytes=64) for xh in range(2)]
        out_scales = keep.tile([P, NODES], U8, name="out_scales", align_bytes=64)
        picked = [keep.tile([P, EDGES], F32, name="picked%d" % j) for j in range(PLANES)]
        both = [keep.tile([P, EDGES], F32, name="both%d" % j) for j in range(PLANES)]
        back = psum.tile([P, NODES], F32, name="back")

        def gather_u(j, first, count):
            window = u_planes[j][:].indirect(entries(lea, first, count))
            nc.vector.tensor_copy(picked[j][:, first : first + count], window)

        def gather_v(j, first, count):
            window = v_planes[j][:].indirect(entries(inn, first, count))
            nc.vector.tensor_tensor(both[j][:, first : first + count], window, picked[j][:, first : first + count], ALU.add)

        def add_pairs_on_tensor(j):
            turned = keep.tile([P, NODES], F32, name="turned%d" % j)
            summed = banks[2 + j % 2]
            for block in range(NODES // P):
                for e in range(2):
                    nc.tensor.matmul(
                        summed[:, block * P : (block + 1) * P],
                        lhsT=both[j][:, 2 * block * P + e : 2 * (block + 1) * P : 2],
                        rhs=ident[:],
                        start=(e == 0),
                        stop=(e == 1),
                        is_transpose=True,
                    )
            nc.scalar.copy(turned[:], summed[:])
            for block in range(NODES // P):
                cols = slice(block * P, (block + 1) * P)
                nc.tensor.transpose(back[:, cols], turned[:, cols], ident[:])
            nc.scalar.copy(result[:, j, :], back[:])

        def finish_nodes(xh):
            nodes = slice(xh * NODE_HALF, (xh + 1) * NODE_HALF)
            pairs = both[LAST][:].rearrange("p (x e) -> p x e", e=2)[:, nodes, :]
            nc.vector.tensor_tensor(result[:, LAST, nodes], pairs[:, :, 0], pairs[:, :, 1], ALU.add)
            nc.sync.dma_start(out_rows[:, 2:4, nodes], result[:, 2:4, nodes])

        def store_planes(xh):
            nodes = slice(xh * NODE_HALF, (xh + 1) * NODE_HALF)
            nc.vector.quantize_mx(out_codes[xh][:].bitcast(E4M3), out_scales[:, nodes], out_words[xh][:])
            nc.sync.dma_start(words_hbm[:, nodes], out_codes[xh][:].bitcast(I32))

        gather_u(0, 0, EDGES)
        gather_u(1, 0, EDGES)
        gather_v(0, 0, EDGES)
        add_pairs_on_tensor(0)
        nc.sync.dma_start(out_rows[:, 0, :], result[:, 0, :])
        gather_u(2, 0, EDGES)
        gather_v(1, 0, EDGES)
        add_pairs_on_tensor(1)
        nc.sync.dma_start(out_rows[:, 1, :], result[:, 1, :])
        gather_v(2, 0, EDGES)
        add_pairs_on_tensor(2)
        for gather in (gather_u, gather_v):
            for xh in range(2):
                gather(LAST, xh * HALF, HALF)

        for xh, copy in enumerate((nc.scalar.copy, nc.vector.tensor_copy)):
            finish_nodes(xh)
            weave(copy, out_words[xh][:], result[:, :, xh * NODE_HALF : (xh + 1) * NODE_HALF])
        for xh in range(2):
            store_planes(xh)
        for quadrant in range(4):
            queue = nc.sync if quadrant % 2 == 0 else nc.scalar
            queue.dma_start(
                scales_hbm[4 * quadrant : 4 * quadrant + 4, :],
                out_scales[32 * quadrant : 32 * quadrant + 4, :].bitcast(I32),
            )
